import numpy as np
import ml_dtypes


def mxq(x, axis, fmt="e4m3"):
    dtype, down = {"e4m3": (ml_dtypes.float8_e4m3fn, 7), "e5m2": (ml_dtypes.float8_e5m2, 14)}[fmt]
    v = np.moveaxis(np.asarray(x, np.float32).astype(ml_dtypes.bfloat16).astype(np.float64), axis, -1)
    blocks = v.reshape(v.shape[:-1] + (-1, 32))
    amax = np.abs(blocks).max(-1, keepdims=True)
    byte = np.maximum(np.where(amax > 0, np.frexp(amax)[1] - 1 + 127, 0) - down, 1)
    scale = np.exp2(byte - 127.0)
    codes = (blocks / scale).astype(np.float32).astype(dtype).astype(np.float64)
    return np.moveaxis((codes * scale).reshape(v.shape), -1, axis)


WIDE = False


def mx_kscale(k):
    if not WIDE:
        return np.ones(k)
    levels = np.array([10, -10, 5, -5, 0])
    if k % 512:
        return np.exp2(np.random.permutation(np.resize(levels, k // 32))).repeat(32)
    a = np.empty((k // 512, 16))
    for p in range(k // 512):
        a[p, :8] = np.random.permutation(np.resize(levels, 8))
        for g in range(8):
            far = levels[np.abs(levels - a[p, g]) >= 10]
            a[p, g + 8] = far[np.random.randint(len(far))]
    return np.exp2(a.ravel()).repeat(32)


def f64(x):
    return np.asarray(x).astype(np.float64)


def striped(idx):
    return np.tile(idx.reshape(-1, 16).T, (8, 1)).astype(np.uint16)


def unstriped(offs):
    return offs[:16].T.reshape(-1).astype(np.int64)


def striped8(idx):
    return np.concatenate([x.reshape(-1, 16).T for x in idx]).astype(np.uint16)


def runs(offs, k):
    lists = np.stack([offs[16 * r : 16 * r + 16].T.reshape(-1) for r in range(8)]).astype(np.int64)
    return lists[np.arange(k) % 512 // 64]


def pack_weight(w):
    k, n = w.shape
    w = f64(np.asarray(w, np.float32).astype(ml_dtypes.bfloat16)).reshape(k // 32, 32, n)
    amax = np.abs(w).max(1)
    byte = np.clip(np.where(amax > 0, np.frexp(amax)[1] - 1 + 127 - 7, 1), 1, 254)
    scaled = (w * np.exp2(127.0 - byte)[:, None, :]).reshape(k, n).astype(np.float32)
    words = np.ascontiguousarray(scaled.reshape(k // 512, 128, 4, n).transpose(0, 1, 3, 2)).astype(ml_dtypes.float8_e4m3fn).view(np.uint8)
    return words, np.ascontiguousarray(byte.astype(np.uint8).reshape(k // 512, 16, n))


def unpack_weight(words, scales):
    g, p, n, _ = words.shape
    vals = np.ascontiguousarray(words).view(ml_dtypes.float8_e4m3fn).astype(np.float64) * np.repeat(np.exp2(scales.astype(np.float64) - 127.0), 8, axis=1)[..., None]
    return vals.transpose(0, 1, 3, 2).reshape(g * 512, n)


K, T, S, N, G, H, J, W = 512, 1024, 512, 512, 2048, 512, 512, 256


def setup_inputs():
    n = np.random.standard_normal
    s = mx_kscale(K)[:, None]
    u = mx_kscale(S)
    packed_xT = pack_weight(n((K, T)) * s)
    packed_dT = pack_weight(n((K, G)) / s)
    perm = np.stack([np.random.permutation(S) for _ in range(8)])
    return {
        "x_words": packed_xT[0],
        "x_scales": packed_xT[1],
        "d_words": packed_dT[0],
        "d_scales": packed_dT[1],
        "tab": n((H, J)).astype(np.float32),
        "gn": (np.random.uniform(0.5, 1.5, (H, 1)) * u[:, None]).astype(np.float32),
        "gm": (np.random.uniform(0.5, 1.5, (H, 1)) * u[:, None]).astype(np.float32),
        "w1": (n((H, N)) / np.sqrt(2 * H) / u[:, None]).astype(np.float32),
        "w2": (n((H, N)) / np.sqrt(2 * H) / u[:, None]).astype(np.float32),
        "offs": striped(np.random.permutation(T)[:S]),
        "k1": striped8(np.random.randint(0, G, (8, H))),
        "two": striped(np.random.permutation(T)[:S]),
        "k2": striped8(np.random.randint(0, G, (8, H))),
        "n1": striped8(np.random.randint(0, J, (8, S))),
        "n2": striped8(np.stack([np.random.permutation(S) for _ in range(8)])),
        "n3": striped8(np.stack([np.random.permutation(S) for _ in range(8)])),
        "n4": striped8(np.stack([np.random.permutation(S) for _ in range(8)])),
        "n5": striped8(perm[:, :W]),
        "n6": striped8(perm[:, W:]),
    }


def reference(x_words, x_scales, d_words, d_scales, tab, gn, gm, w1, w2, offs, k1, two, k2, n1, n2, n3, n4, n5, n6):
    d_k1 = unpack_weight(d_words, d_scales)[np.arange(K)[:, None], runs(k1, K)]
    xq = unpack_weight(x_words, x_scales)[:, unstriped(offs)]
    a = 0.0625 * (d_k1.T @ xq)
    z = f64(gn) * (np.maximum(a + f64(tab)[np.arange(H)[:, None], runs(n1, H)], a[np.arange(H)[:, None], runs(n2, H)]))
    d_k2 = unpack_weight(d_words, d_scales)[np.arange(K)[:, None], runs(k2, K)]
    x_two = unpack_weight(x_words, x_scales)[:, unstriped(two)]
    b = 0.0625 * (d_k2.T @ x_two)
    sq = (b) ** 2
    z2 = f64(gm) * ((b[np.arange(H)[:, None], runs(n4, H)]) / (np.sqrt(sq + sq[np.arange(H)[:, None], runs(n3, H)] + 0.25)))
    h = mxq(f64(w1), 0, "e4m3").T @ mxq(z, 0, "e4m3") + mxq(f64(w2), 0, "e4m3").T @ mxq(z2, 0, "e4m3")
    pa = h[np.arange(N)[:, None], runs(n5, N)]
    pb = h[np.arange(N)[:, None], runs(n6, N)]
    rb = np.maximum(pa, pb)
    ra = pa / (np.abs(pb) + 0.5)
    ds = np.zeros((N, S))
    ds[np.arange(N)[:, None], runs(n5, N)] = ra
    out = ds.copy()
    out[np.arange(N)[:, None], runs(n6, N)] = rb
    return out

@@ -1,0 +1,267 @@
+from contextlib import ExitStack
+
+import concourse.mybir as mybir
+
+F32 = mybir.dt.float32
+BF16 = mybir.dt.bfloat16
+I32 = mybir.dt.int32
+U32 = mybir.dt.uint32
+U16 = mybir.dt.uint16
+U8 = mybir.dt.uint8
+FP8X4 = mybir.dt.float8_e4m3fn_x4
+ALU = mybir.AluOpType
+ACT = mybir.ActivationFunctionType
+
+P = 128
+PACK = 4
+K, T, G, H, S, N, W = 512, 1024, 2048, 512, 512, 512, 256
+HALF = S // 2
+GROUP = 16
+FLOPS = 4 * 2 * 512 * 512 * 512
+
+
+def tile_picked_pqjkindrmsratio_none_p_kernel(
+    tc, x_words, x_scales, d_words, d_scales, tab, gn, gm, w1, w2, offs, k1, two, k2, n1, n2, n3, n4, n5, n6, out
+):
+    nc = tc.nc
+    with ExitStack() as ctx:
+        lists = ctx.enter_context(tc.tile_pool(name="lists", bufs=1))
+        keep = ctx.enter_context(tc.tile_pool(name="keep", bufs=1))
+        psum = ctx.enter_context(tc.psum_pool(name="psum", bufs=1))
+
+        def sb(name, shape, dtype):
+            return keep.tile(shape, dtype, name=name, align_bytes=64)
+
+        def load_list(name, src):
+            tile = lists.tile([P, src.shape[1]], U16, name=name)
+            nc.sync.dma_start(tile[:], src)
+            return tile
+
+        def half_of(tile, c):
+            return tile[:, c * (HALF // GROUP) : (c + 1) * (HALF // GROUP)]
+
+        d_byte_win = sb("d_byte_win", [P, G], U8)
+        x_byte_win = sb("x_byte_win", [P, T], U8)
+        nc.vector.memset(d_byte_win[:].bitcast(I32), 0)
+        nc.vector.memset(x_byte_win[:].bitcast(I32), 0)
+        tab_rows = tab.rearrange("(p t) j -> t p j", t=PACK)
+        tab_win = [sb(f"tab_win{t}", [P, S], F32) for t in range(PACK)]
+        k2_t = load_list("k2_t", k2)
+        nc.sync.dma_start(tab_win[0][:], tab_rows[0])
+        d_rows = d_scales[0].bitcast(I32).rearrange("(r e) c -> e r c", e=2)
+        for e in range(2):
+            nc.sync.dma_start(d_byte_win[e:P:GROUP, :].bitcast(I32), d_rows[e])
+        k1_t = load_list("k1_t", k1)
+        n1_t = load_list("n1_t", n1)
+        nc.sync.dma_start(tab_win[1][:], tab_rows[1])
+        d_word_win = sb("d_word_win", [P, G], I32)
+        nc.sync.dma_start(d_word_win[:], d_words[0].rearrange("p c r -> p (c r)").bitcast(I32))
+        two_t = load_list("two_t", two)
+        x_rows = x_scales[0].bitcast(I32).rearrange("(q r) c -> r q c", r=4)
+        for r in range(4):
+            nc.sync.dma_start(x_byte_win[r:P:32, :].bitcast(I32), x_rows[r])
+        for t in range(2, PACK):
+            nc.sync.dma_start(tab_win[t][:], tab_rows[t])
+        x_word_win = sb("x_word_win", [P, T], I32)
+        nc.sync.dma_start(x_word_win[:], x_words[0].rearrange("p c r -> p (c r)").bitcast(I32))
+        gm_t = sb("gm_t", [P, PACK], F32)
+        nc.sync.dma_start(gm_t[:], gm.rearrange("(p t) o -> p (t o)", t=PACK))
+        gn_t = sb("gn_t", [P, PACK], F32)
+        nc.sync.dma_start(gn_t[:], gn.rearrange("(p t) o -> p (t o)", t=PACK))
+        offs_t = load_list("offs_t", offs)
+
+        d_bytes = keep.tile([P, 2 * H], U8, name="d_bytes", tag="shared", align_bytes=64)
+        for number, codes_t in enumerate((k2_t, k1_t)):
+            nc.vector.tensor_copy(d_bytes[:, number * H : (number + 1) * H], d_byte_win[:].indirect(codes_t[:]))
+        d_scale = sb("d_scale", [P, 2 * H], U8)
+        nc.vector.tensor_copy(
+            d_scale[:].rearrange("p (l t m) -> p l t m", l=2, t=PACK),
+            d_bytes[:].rearrange("p (l m t) -> p l t m", l=2, t=PACK),
+        )
+        for e in range(2):
+            nc.sync.dma_start(d_scale[2 + e : P : 32, :].bitcast(I32), d_scale[GROUP + e : P : 32, :].bitcast(I32))
+        w_raw = keep.tile([P, 2, PACK, N], F32, name="w_raw", tag="shared", align_bytes=64)
+        w1_raw, w2_raw = w_raw[:, 0], w_raw[:, 1]
+        nc.sync.dma_start(w2_raw, w2.rearrange("(p j) m -> p j m", j=PACK))
+        nc.sync.dma_start(w1_raw, w1.rearrange("(p j) m -> p j m", j=PACK))
+        n3_t = load_list("n3_t", n3)
+        n4_t = load_list("n4_t", n4)
+        n2_t = load_list("n2_t", n2)
+        n5_t = load_list("n5_t", n5)
+        n6_t = load_list("n6_t", n6)
+
+        def coded_product(name, number, codes_t, tokens_t):
+            d_picked = sb(name + "_d_picked", [P, H], U32)
+            nc.vector.tensor_copy(d_picked[:], d_word_win[:].bitcast(U32).indirect(codes_t[:]))
+            x_scale = sb(name + "_x_scale", [P, S], U8)
+            nc.vector.tensor_copy(x_scale[:], x_byte_win[:].indirect(tokens_t[:]))
+            d_dealt = sb(name + "_d_dealt", [P, H], U32)
+            nc.vector.tensor_copy(
+                d_dealt[:].rearrange("p (t m) -> p m t", t=PACK), d_picked[:].rearrange("p (m t) -> p m t", t=PACK)
+            )
+            x_picked = sb(name + "_x_picked", [P, S], U32)
+            nc.vector.tensor_copy(x_picked[:], x_word_win[:].bitcast(U32).indirect(tokens_t[:]))
+            banks = []
+            for t in range(PACK):
+                bank = psum.tile([P, S], F32, name=f"{name}_bank{t}", tag=f"bank{number * PACK + t}")
+                nc.tensor.matmul_mx(
+                    bank[:], lhsT=d_dealt[:, t * P : (t + 1) * P].bitcast(FP8X4),
+                    lhsT_scale=d_scale[:, number * H + t * P : number * H + (t + 1) * P],
+                    rhs=x_picked[:].bitcast(FP8X4), rhs_scale=x_scale[:], start=True, stop=True,
+                )
+                banks.append(bank)
+            return banks
+
+        def gather_scalar(dst, window, offsets):
+            nc.scalar.activation(dst, window[:].indirect(offsets), ACT.Copy)
+
+        def gather_vector(dst, window, offsets):
+            nc.vector.tensor_copy(dst, window[:].indirect(offsets))
+
+        tab_g = [sb(f"tab_g{t}", [P, S], F32) for t in range(PACK)]
+
+        def gather_tab(t):
+            for c in range(2):
+                gather_scalar(tab_g[t][:, c * HALF : (c + 1) * HALF], tab_win[t], half_of(n1_t, c))
+
+        for t in range(PACK):
+            gather_tab(t)
+        b_banks = coded_product("b", 0, k2_t, two_t)
+
+        gm16 = sb("gm16", [P, PACK], F32)
+        nc.vector.tensor_scalar(gm16[:], gm_t[:], 0.0625, None, ALU.mult)
+        sign = sb("sign", [P, PACK], F32)
+        step = sb("step", [P, PACK], F32)
+        nc.vector.tensor_scalar(step[:], gn_t[:], 0.0, 2.0, ALU.is_ge, ALU.mult)
+        nc.vector.tensor_scalar(sign[:], step[:], -1.0, None, ALU.add)
+        size = sb("size", [P, PACK], F32)
+        nc.vector.tensor_tensor(size[:], gn_t[:], sign[:], ALU.mult)
+        size16 = sb("size16", [P, PACK], F32)
+        nc.vector.tensor_scalar(size16[:], size[:], 0.0625, None, ALU.mult)
+
+        a_banks = coded_product("a", 1, k1_t, offs_t)
+
+        sq_win = [sb(f"sq_win{t}", [P, S], F32) for t in range(PACK)]
+        b_win = [sb(f"b_win{t}", [P, S], F32) for t in range(PACK)]
+        sq_g = [sb(f"sq_g{t}", [P, S], F32) for t in range(PACK)]
+        a_win = [sb(f"a_win{t}", [P, S], F32) for t in range(PACK)]
+        for t in range(PACK):
+            nc.scalar.activation(sq_win[t][:], b_banks[t][:], ACT.Square, scale=0.0625)
+        for t in range(PACK):
+            if t == 2:
+                for u in range(PACK):
+                    nc.scalar.activation(a_win[u][:], a_banks[u][:], ACT.Copy, scale=size16[:, u : u + 1])
+            for c in range(2):
+                gather_scalar(sq_g[t][:, c * HALF : (c + 1) * HALF], sq_win[t], half_of(n3_t, c))
+        for t in range(PACK):
+            nc.scalar.activation(b_win[t][:], b_banks[t][:], ACT.Copy, scale=gm16[:, t : t + 1])
+
+        def quantised(name, grouped, width):
+            codes = sb(name + "_codes", [P, width], U32)
+            scale = sb(name + "_scale", [P, width], U8)
+            nc.vector.quantize_mx(out=codes[:].bitcast(FP8X4), scales=scale[:], in_=grouped[:])
+            return codes, scale
+
+        w2_grouped = sb("w2_grouped", [P, N * PACK], BF16)
+        w1_grouped = sb("w1_grouped", [P, N * PACK], BF16)
+        nc.vector.tensor_copy(
+            w2_grouped[:].rearrange("p (t m j) -> p m j t", t=PACK, j=PACK),
+            w2_raw.rearrange("p j (m t) -> p m j t", t=PACK),
+        )
+        nc.vector.tensor_tensor(
+            w1_grouped[:].rearrange("p (t m j) -> p m j t", t=PACK, j=PACK),
+            w1_raw.rearrange("p j (m t) -> p m j t", t=PACK),
+            sign[:].unsqueeze(1).unsqueeze(3).to_broadcast([P, P, PACK, PACK]),
+            ALU.mult,
+        )
+        w2_codes, w2_scale = quantised("w2", w2_grouped, N)
+        w1_codes, w1_scale = quantised("w1", w1_grouped, N)
+
+        def weave(name, left, right, op):
+            grouped = sb(name + "_grouped", [P, HALF * PACK], BF16)
+            nc.vector.tensor_tensor(
+                grouped[:].rearrange("p (c i t) -> p c t i", i=4, t=PACK),
+                left[:].rearrange("p t (c i) -> p c t i", i=4),
+                right[:].rearrange("p t (c i) -> p c t i", i=4),
+                op,
+            )
+            return grouped
+
+        first = [sb(f"first{c}", [P, PACK, HALF], F32) for c in range(2)]
+        a_g = [sb(f"a_g{c}", [P, PACK, HALF], F32) for c in range(2)]
+        b_g = [sb(f"b_g{c}", [P, PACK, HALF], F32) for c in range(2)]
+        root = [sb(f"root{c}", [P, PACK, HALF], F32) for c in range(2)]
+        total = [sb(f"total{t}", [P, S], F32) for t in range(PACK)]
+        for t in range(PACK):
+            nc.vector.tensor_tensor(total[t][:], sq_g[t][:], sq_win[t][:], ALU.add)
+        for c in range(2):
+            for t in range(PACK):
+                cols = slice(c * HALF, (c + 1) * HALF)
+                nc.vector.scalar_tensor_tensor(
+                    first[c][:, t, :], tab_g[t][:, cols], size[:, t : t + 1], a_win[t][:, cols], ALU.mult, ALU.add
+                )
+        for t in range(PACK):
+            gather_vector(a_g[0][:, t, :], a_win[t], half_of(n2_t, 0))
+        for c in range(2):
+            for t in range(PACK):
+                nc.scalar.activation(
+                    root[c][:, t, :], total[t][:, c * HALF : (c + 1) * HALF], ACT.Abs_reciprocal_sqrt, bias=0.25
+                )
+                gather_scalar(b_g[c][:, t, :], b_win[t], half_of(n4_t, c))
+        z_grouped0 = weave("z0", first[0], a_g[0], ALU.max)
+        for t in range(2):
+            gather_vector(a_g[1][:, t, :], a_win[t], half_of(n2_t, 1))
+        z_q = [quantised("z0", z_grouped0, HALF)]
+        z2_grouped0 = weave("y0", b_g[0], root[0], ALU.mult)
+        for t in range(2, PACK):
+            gather_scalar(a_g[1][:, t, :], a_win[t], half_of(n2_t, 1))
+        z2_q = [quantised("y0", z2_grouped0, HALF)]
+        z2_grouped1 = weave("y1", b_g[1], root[1], ALU.mult)
+        z_grouped1 = weave("z1", first[1], a_g[1], ALU.max)
+        z2_q.append(quantised("y1", z2_grouped1, HALF))
+        z_q.append(quantised("z1", z_grouped1, HALF))
+
+        h_banks = []
+        h_win = [sb(f"h_win{t}", [P, S], F32) for t in range(PACK)]
+        for c in range(2):
+            for t in range(PACK):
+                cols = slice(t * P, (t + 1) * P)
+                h_bank = psum.tile([P, HALF], F32, name=f"h_bank{c}{t}", tag=f"bank{(1 - c) * PACK + t}")
+                for number, (w_codes, w_scale, moving) in enumerate(((w2_codes, w2_scale, z2_q), (w1_codes, w1_scale, z_q))):
+                    nc.tensor.matmul_mx(
+                        h_bank[:], lhsT=w_codes[:, cols].bitcast(FP8X4), lhsT_scale=w_scale[:, cols],
+                        rhs=moving[c][0][:].bitcast(FP8X4), rhs_scale=moving[c][1][:],
+                        start=(number == 0), stop=(number == 1),
+                    )
+                if c == 0:
+                    nc.scalar.activation(h_win[t][:, :HALF], h_bank[:], ACT.Copy)
+                else:
+                    h_banks.append(h_bank)
+
+        out_rows = out.rearrange("(p t) j -> t p j", t=PACK)
+        pa, pb, inv, larger, result = [], [], [], [], []
+        for t in range(PACK):
+            nc.scalar.activation(h_win[t][:, HALF:], h_banks[t][:], ACT.Copy)
+            pa.append(sb(f"pa{t}", [P, W], F32))
+            pb.append(sb(f"pb{t}", [P, W], F32))
+            gather_scalar(pb[t][:], h_win[t], n6_t[:])
+            (gather_vector if t == 0 else gather_scalar)(pa[t][:], h_win[t], n5_t[:])
+            pb_size = sb(f"pb_size{t}", [P, W], F32)
+            nc.scalar.activation(pb_size[:], pb[t][:], ACT.Abs)
+            inv_root = sb(f"inv_root{t}", [P, W], F32)
+            nc.scalar.activation(inv_root[:], pb_size[:], ACT.Abs_reciprocal_sqrt, bias=0.5)
+            inv.append(sb(f"inv{t}", [P, W], F32))
+            nc.scalar.activation(inv[t][:], inv_root[:], ACT.Square)
+            larger.append(sb(f"larger{t}", [P, W], F32))
+            result.append(sb(f"result{t}", [P, S], F32))
+
+        def finish(t):
+            nc.vector.tensor_tensor(result[t][:].indirect(n5_t[:]), pa[t][:], inv[t][:], ALU.mult)
+            nc.sync.dma_start(out_rows[t], result[t][:])
+
+        for t in range(PACK):
+            nc.vector.tensor_tensor(larger[t][:], pa[t][:], pb[t][:], ALU.max)
+            if t > 0:
+                finish(t - 1)
+            nc.vector.tensor_copy(result[t][:].indirect(n6_t[:]), larger[t][:])
+        finish(PACK - 1)

@@ -1,6 +1,7 @@
 from contextlib import ExitStack
 
 import concourse.mybir as mybir
+from concourse.masks import make_identity
 
 F32 = mybir.dt.float32
 BF16 = mybir.dt.bfloat16
@@ -40,74 +41,78 @@ def tile_picked_pqjkindrmsratio_none_p_kernel(
         def half_of(tile, c):
             return tile[:, c * (HALF // GROUP) : (c + 1) * (HALF // GROUP)]
 
+        warm = sb("warm", [P, 2], F32)
+        nc.gpsimd.memset(warm[:, 0:1], 1.0)
+        nc.scalar.activation(warm[:, 1:2], warm[:, 0:1], ACT.Abs_reciprocal_sqrt, bias=0.25)
         d_byte_win = sb("d_byte_win", [P, G], U8)
         x_byte_win = sb("x_byte_win", [P, T], U8)
         nc.vector.memset(d_byte_win[:].bitcast(I32), 0)
         nc.vector.memset(x_byte_win[:].bitcast(I32), 0)
         tab_rows = tab.rearrange("(p t) j -> t p j", t=PACK)
         tab_win = [sb(f"tab_win{t}", [P, S], F32) for t in range(PACK)]
+        gm_t = sb("gm_t", [P, PACK], F32)
+        nc.gpsimd.dma_start(gm_t[:], gm.rearrange("(p t) o -> p (t o)", t=PACK))
+        gn_t = sb("gn_t", [P, PACK], F32)
+        nc.gpsimd.dma_start(gn_t[:], gn.rearrange("(p t) o -> p (t o)", t=PACK))
         k2_t = load_list("k2_t", k2)
-        nc.sync.dma_start(tab_win[0][:], tab_rows[0])
-        d_rows = d_scales[0].bitcast(I32).rearrange("(r e) c -> e r c", e=2)
-        for e in range(2):
-            nc.sync.dma_start(d_byte_win[e:P:GROUP, :].bitcast(I32), d_rows[e])
-        k1_t = load_list("k1_t", k1)
+        two_t = load_list("two_t", two)
         n1_t = load_list("n1_t", n1)
-        nc.sync.dma_start(tab_win[1][:], tab_rows[1])
+        nc.sync.dma_start(d_byte_win[0:P:8, :].bitcast(I32), d_scales[0].bitcast(I32))
+        nc.sync.dma_start(x_byte_win[0:P:8, :].bitcast(I32), x_scales[0].bitcast(I32))
+        nc.sync.dma_start(tab_win[0][:], tab_rows[0])
         d_word_win = sb("d_word_win", [P, G], I32)
         nc.sync.dma_start(d_word_win[:], d_words[0].rearrange("p c r -> p (c r)").bitcast(I32))
-        two_t = load_list("two_t", two)
-        x_rows = x_scales[0].bitcast(I32).rearrange("(q r) c -> r q c", r=4)
-        for r in range(4):
-            nc.sync.dma_start(x_byte_win[r:P:32, :].bitcast(I32), x_rows[r])
-        for t in range(2, PACK):
-            nc.sync.dma_start(tab_win[t][:], tab_rows[t])
+        nc.sync.dma_start(tab_win[1][:], tab_rows[1])
         x_word_win = sb("x_word_win", [P, T], I32)
         nc.sync.dma_start(x_word_win[:], x_words[0].rearrange("p c r -> p (c r)").bitcast(I32))
-        gm_t = sb("gm_t", [P, PACK], F32)
-        nc.sync.dma_start(gm_t[:], gm.rearrange("(p t) o -> p (t o)", t=PACK))
-        gn_t = sb("gn_t", [P, PACK], F32)
-        nc.sync.dma_start(gn_t[:], gn.rearrange("(p t) o -> p (t o)", t=PACK))
+        k1_t = load_list("k1_t", k1)
         offs_t = load_list("offs_t", offs)
-
-        d_bytes = keep.tile([P, 2 * H], U8, name="d_bytes", tag="shared", align_bytes=64)
-        for number, codes_t in enumerate((k2_t, k1_t)):
-            nc.vector.tensor_copy(d_bytes[:, number * H : (number + 1) * H], d_byte_win[:].indirect(codes_t[:]))
-        d_scale = sb("d_scale", [P, 2 * H], U8)
-        nc.vector.tensor_copy(
-            d_scale[:].rearrange("p (l t m) -> p l t m", l=2, t=PACK),
-            d_bytes[:].rearrange("p (l m t) -> p l t m", l=2, t=PACK),
-        )
-        for e in range(2):
-            nc.sync.dma_start(d_scale[2 + e : P : 32, :].bitcast(I32), d_scale[GROUP + e : P : 32, :].bitcast(I32))
-        w_raw = keep.tile([P, 2, PACK, N], F32, name="w_raw", tag="shared", align_bytes=64)
-        w1_raw, w2_raw = w_raw[:, 0], w_raw[:, 1]
-        nc.sync.dma_start(w2_raw, w2.rearrange("(p j) m -> p j m", j=PACK))
-        nc.sync.dma_start(w1_raw, w1.rearrange("(p j) m -> p j m", j=PACK))
         n3_t = load_list("n3_t", n3)
-        n4_t = load_list("n4_t", n4)
+        nc.sync.dma_start(tab_win[2][:], tab_rows[2])
+
+        def picked_scales(name, codes_t, tokens_t, queues):
+            d_bytes = sb(name + "_d_bytes", [P, H], U8)
+            nc.vector.tensor_copy(d_bytes[:], d_byte_win[:].indirect(codes_t[:]))
+            x_bytes = keep.tile([P, S], U8, name=name + "_x_bytes", tag=name + "_shared", align_bytes=64)
+            nc.vector.tensor_copy(x_bytes[:], x_byte_win[:].indirect(tokens_t[:]))
+            scale = sb(name + "_scale", [P, H + S], U8)
+            nc.vector.tensor_copy(
+                scale[:, :H].rearrange("p (t m) -> p t m", t=PACK), d_bytes[:].rearrange("p (m t) -> p t m", t=PACK)
+            )
+            nc.vector.tensor_copy(scale[:, H:].bitcast(I32), x_bytes[:].bitcast(I32))
+            for r in range(1, 4):
+                queues[r - 1].dma_start(scale[r:P:32, :].bitcast(I32), scale[8 * r : P : 32, :].bitcast(I32))
+            return scale
+
+        def load_weight(name, src, tag):
+            tile = keep.tile([P, PACK * N], F32, name=name, tag=tag, align_bytes=64)
+            raw = tile[:].rearrange("p (j m) -> p j m", j=PACK)
+            nc.sync.dma_start(raw, src.rearrange("(p j) m -> p j m", j=PACK))
+            return raw
+
+        b_scale = picked_scales("b", k2_t, two_t, (nc.gpsimd, nc.scalar, nc.scalar))
+        nc.sync.dma_start(tab_win[3][:], tab_rows[3])
+        w1_raw = load_weight("w1_raw", w1, "b_shared")
         n2_t = load_list("n2_t", n2)
+        n4_t = load_list("n4_t", n4)
         n5_t = load_list("n5_t", n5)
         n6_t = load_list("n6_t", n6)
 
-        def coded_product(name, number, codes_t, tokens_t):
+        def coded_product(name, number, scale, codes_t, tokens_t):
             d_picked = sb(name + "_d_picked", [P, H], U32)
             nc.vector.tensor_copy(d_picked[:], d_word_win[:].bitcast(U32).indirect(codes_t[:]))
-            x_scale = sb(name + "_x_scale", [P, S], U8)
-            nc.vector.tensor_copy(x_scale[:], x_byte_win[:].indirect(tokens_t[:]))
+            x_picked = sb(name + "_x_picked", [P, S], U32)
+            nc.vector.tensor_copy(x_picked[:], x_word_win[:].bitcast(U32).indirect(tokens_t[:]))
             d_dealt = sb(name + "_d_dealt", [P, H], U32)
             nc.vector.tensor_copy(
                 d_dealt[:].rearrange("p (t m) -> p m t", t=PACK), d_picked[:].rearrange("p (m t) -> p m t", t=PACK)
             )
-            x_picked = sb(name + "_x_picked", [P, S], U32)
-            nc.vector.tensor_copy(x_picked[:], x_word_win[:].bitcast(U32).indirect(tokens_t[:]))
             banks = []
             for t in range(PACK):
                 bank = psum.tile([P, S], F32, name=f"{name}_bank{t}", tag=f"bank{number * PACK + t}")
                 nc.tensor.matmul_mx(
-                    bank[:], lhsT=d_dealt[:, t * P : (t + 1) * P].bitcast(FP8X4),
-                    lhsT_scale=d_scale[:, number * H + t * P : number * H + (t + 1) * P],
-                    rhs=x_picked[:].bitcast(FP8X4), rhs_scale=x_scale[:], start=True, stop=True,
+                    bank[:], lhsT=d_dealt[:, t * P : (t + 1) * P].bitcast(FP8X4), lhsT_scale=scale[:, t * P : (t + 1) * P],
+                    rhs=x_picked[:].bitcast(FP8X4), rhs_scale=scale[:, H:], start=True, stop=True,
                 )
                 banks.append(bank)
             return banks
@@ -126,142 +131,218 @@ def tile_picked_pqjkindrmsratio_none_p_kernel(
 
         for t in range(PACK):
             gather_tab(t)
-        b_banks = coded_product("b", 0, k2_t, two_t)
+        b_banks = coded_product("b", 0, b_scale, k2_t, two_t)
 
+        identity = sb("identity", [P, P], F32)
+        make_identity(nc, identity[:])
         gm16 = sb("gm16", [P, PACK], F32)
-        nc.vector.tensor_scalar(gm16[:], gm_t[:], 0.0625, None, ALU.mult)
+        nc.gpsimd.tensor_scalar(gm16[:], gm_t[:], 0.0625, 0.0, ALU.mult, ALU.add)
         sign = sb("sign", [P, PACK], F32)
         step = sb("step", [P, PACK], F32)
-        nc.vector.tensor_scalar(step[:], gn_t[:], 0.0, 2.0, ALU.is_ge, ALU.mult)
-        nc.vector.tensor_scalar(sign[:], step[:], -1.0, None, ALU.add)
+        nc.gpsimd.tensor_scalar(step[:], gn_t[:], 0.0, 2.0, ALU.is_ge, ALU.mult)
+        nc.gpsimd.tensor_scalar(sign[:], step[:], 1.0, -1.0, ALU.mult, ALU.add)
         size = sb("size", [P, PACK], F32)
-        nc.vector.tensor_tensor(size[:], gn_t[:], sign[:], ALU.mult)
+        nc.gpsimd.tensor_tensor(size[:], gn_t[:], sign[:], ALU.mult)
         size16 = sb("size16", [P, PACK], F32)
-        nc.vector.tensor_scalar(size16[:], size[:], 0.0625, None, ALU.mult)
+        nc.gpsimd.tensor_scalar(size16[:], size[:], 0.0625, 0.0, ALU.mult, ALU.add)
 
-        a_banks = coded_product("a", 1, k1_t, offs_t)
+        a_scale = picked_scales("a", k1_t, offs_t, (nc.sync, nc.sync, nc.sync))
+        w2_raw = load_weight("w2_raw", w2, "a_shared")
+        a_banks = coded_product("a", 1, a_scale, k1_t, offs_t)
+
+        w2_grouped = sb("w2_grouped", [P, N * PACK], BF16)
+        w1_grouped = sb("w1_grouped", [P, N * PACK], BF16)
+        PIECE = 64
+        for t in range(PACK):
+            for m0 in range(0, P, PIECE):
+                nc.gpsimd.tensor_tensor(
+                    w1_grouped[:].rearrange("p (t m j) -> p t m j", t=PACK, j=PACK)[:, t, m0 : m0 + PIECE],
+                    w1_raw.rearrange("p j (m t) -> p t m j", t=PACK)[:, t, m0 : m0 + PIECE],
+                    sign[:].unsqueeze(1).to_broadcast([P, PIECE, PACK]),
+                    ALU.mult,
+                )
+        for t in range(PACK):
+            for m0 in range(0, P, PIECE):
+                nc.gpsimd.tensor_scalar(
+                    w2_grouped[:].rearrange("p (t m j) -> p t m j", t=PACK, j=PACK)[:, t, m0 : m0 + PIECE],
+                    w2_raw.rearrange("p j (m t) -> p t m j", t=PACK)[:, t, m0 : m0 + PIECE],
+                    1.0, 0.0, ALU.mult, ALU.add,
+                )
+
+        def quantised(name, grouped, width):
+            codes = sb(name + "_codes", [P, width], U32)
+            scale = sb(name + "_scale", [P, width], U8)
+            nc.vector.quantize_mx(out=codes[:].bitcast(FP8X4), scales=scale[:], in_=grouped)
+            return codes, scale
+
+        def weave(grouped, left, right, op):
+            nc.vector.tensor_tensor(
+                grouped.rearrange("p (c i t) -> p c t i", i=4, t=PACK),
+                left.rearrange("p t (c i) -> p c t i", i=4),
+                right.rearrange("p t (c i) -> p c t i", i=4),
+                op,
+            )
+
+        def cols_of(c):
+            return slice(c * HALF, (c + 1) * HALF)
 
         sq_win = [sb(f"sq_win{t}", [P, S], F32) for t in range(PACK)]
         b_win = [sb(f"b_win{t}", [P, S], F32) for t in range(PACK)]
         sq_g = [sb(f"sq_g{t}", [P, S], F32) for t in range(PACK)]
         a_win = [sb(f"a_win{t}", [P, S], F32) for t in range(PACK)]
+        a_g = [sb("a_g0", [P, PACK, HALF], F32)]
+        b_g = [sb(f"b_g{c}", [P, PACK, HALF], F32) for c in range(2)]
+
+        z_grouped = [sb(f"z_grouped{c}", [P, HALF * PACK], BF16) for c in range(2)]
+        z2_grouped = [sb(f"z2_grouped{c}", [P, HALF * PACK], BF16) for c in range(2)]
+        root_turned = [sb(f"root_turned{t}", [P, S], F32) for t in range(PACK)]
+
+        def block(u):
+            return slice(u * P, (u + 1) * P)
+
+        def make_root(t):
+            total = psum.tile([P, S], F32, name=f"total{t}", tag=f"bank{t}")
+            for u in range(PACK):
+                for number, term in enumerate((sq_win[t], sq_g[t])):
+                    nc.tensor.matmul(
+                        total[:, block(u)], term[:, block(u)], identity[:], start=(number == 0), stop=(number == 1), is_transpose=True
+                    )
+            nc.scalar.activation(root_turned[t][:], total[:], ACT.Abs_reciprocal_sqrt, bias=0.25)
+
+        def weave_z2(c):
+            for v in range(2):
+                weave(z2_grouped[c][:, v * P * PACK : (v + 1) * P * PACK], b_g[c][:, :, block(v)], root[2 * c + v][:], ALU.mult)
+
         for t in range(PACK):
             nc.scalar.activation(sq_win[t][:], b_banks[t][:], ACT.Square, scale=0.0625)
         for t in range(PACK):
-            if t == 2:
-                for u in range(PACK):
-                    nc.scalar.activation(a_win[u][:], a_banks[u][:], ACT.Copy, scale=size16[:, u : u + 1])
-            for c in range(2):
-                gather_scalar(sq_g[t][:, c * HALF : (c + 1) * HALF], sq_win[t], half_of(n3_t, c))
-        for t in range(PACK):
             nc.scalar.activation(b_win[t][:], b_banks[t][:], ACT.Copy, scale=gm16[:, t : t + 1])
-
-        def quantised(name, grouped, width):
-            codes = sb(name + "_codes", [P, width], U32)
-            scale = sb(name + "_scale", [P, width], U8)
-            nc.vector.quantize_mx(out=codes[:].bitcast(FP8X4), scales=scale[:], in_=grouped[:])
-            return codes, scale
-
-        w2_grouped = sb("w2_grouped", [P, N * PACK], BF16)
-        w1_grouped = sb("w1_grouped", [P, N * PACK], BF16)
-        nc.vector.tensor_copy(
-            w2_grouped[:].rearrange("p (t m j) -> p m j t", t=PACK, j=PACK),
-            w2_raw.rearrange("p j (m t) -> p m j t", t=PACK),
-        )
-        nc.vector.tensor_tensor(
-            w1_grouped[:].rearrange("p (t m j) -> p m j t", t=PACK, j=PACK),
-            w1_raw.rearrange("p j (m t) -> p m j t", t=PACK),
-            sign[:].unsqueeze(1).unsqueeze(3).to_broadcast([P, P, PACK, PACK]),
-            ALU.mult,
-        )
-        w2_codes, w2_scale = quantised("w2", w2_grouped, N)
-        w1_codes, w1_scale = quantised("w1", w1_grouped, N)
-
-        def weave(name, left, right, op):
-            grouped = sb(name + "_grouped", [P, HALF * PACK], BF16)
-            nc.vector.tensor_tensor(
-                grouped[:].rearrange("p (c i t) -> p c t i", i=4, t=PACK),
-                left[:].rearrange("p t (c i) -> p c t i", i=4),
-                right[:].rearrange("p t (c i) -> p c t i", i=4),
-                op,
+        for t in range(PACK):
+            nc.scalar.activation(a_win[t][:], a_banks[t][:], ACT.Copy, scale=size16[:, t : t + 1])
+        for t in range(PACK):
+            for c in range(2):
+                gather_vector(sq_g[t][:, cols_of(c)], sq_win[t], half_of(n3_t, c))
+        for t in range(PACK):
+            gather_scalar(b_g[0][:, t, :], b_win[t], half_of(n4_t, 0))
+        for t in range(PACK):
+            (gather_vector if t < 3 else gather_scalar)(a_g[0][:, t, :], a_win[t], half_of(n2_t, 0))
+        for t in range(PACK):
+            make_root(t)
+        root = [psum.tile([P, PACK, P], F32, name=f"root{u}", tag=f"bank{PACK + u}") for u in range(PACK)]
+        for u in range(PACK):
+            for t in range(PACK):
+                nc.tensor.transpose(root[u][:, t, :], root_turned[t][:, block(u)], identity[:])
+        first = keep.tile([P, PACK, S], F32, name="first", tag="first1", align_bytes=64)
+        for t in range(PACK):
+            nc.vector.scalar_tensor_tensor(first[:, t, :], tab_g[t][:], size[:, t : t + 1], a_win[t][:], ALU.mult, ALU.add)
+        weave(z_grouped[0][:], first[:, :, :HALF], a_g[0][:], ALU.max)
+        z_q = [quantised("z0", z_grouped[0][:], HALF)]
+        w1_head = quantised("w1_head", w1_grouped[:, : P * PACK], P)
+        weave_z2(0)
+        w2_head = quantised("w2_head", w2_grouped[:, : P * PACK], P)
+        z2_q = [quantised("y0", z2_grouped[0][:], HALF)]
+        for t in range(PACK):
+            gather_scalar(b_g[1][:, t, :], b_win[t], half_of(n4_t, 1))
+        a_late = [sb(f"a_late{v}", [P, PACK, P], F32) for v in range(2)]
+        for v in range(2):
+            for t in range(PACK):
+                gather_scalar(a_late[v][:, t, :], a_win[t], n2_t[:, (HALF + v * P) // GROUP : (HALF + (v + 1) * P) // GROUP])
+        weave_z2(1)
+        z2_q.append(quantised("y1", z2_grouped[1][:], HALF))
+        z1_codes = sb("z1_codes", [P, HALF], U32)
+        z1_scale = sb("z1_scale", [P, HALF], U8)
+        for v in range(2):
+            weave(z_grouped[1][:, v * P * PACK : (v + 1) * P * PACK], first[:, :, block(2 + v)], a_late[v][:], ALU.max)
+        for v in range(2):
+            nc.vector.quantize_mx(
+                out=z1_codes[:, block(v)].bitcast(FP8X4), scales=z1_scale[:, block(v)], in_=z_grouped[1][:, v * P * PACK : (v + 1) * P * PACK]
             )
-            return grouped
+        z_q.append((z1_codes, z1_scale))
 
-        first = [sb(f"first{c}", [P, PACK, HALF], F32) for c in range(2)]
-        a_g = [sb(f"a_g{c}", [P, PACK, HALF], F32) for c in range(2)]
-        b_g = [sb(f"b_g{c}", [P, PACK, HALF], F32) for c in range(2)]
-        root = [sb(f"root{c}", [P, PACK, HALF], F32) for c in range(2)]
-        total = [sb(f"total{t}", [P, S], F32) for t in range(PACK)]
-        for t in range(PACK):
-            nc.vector.tensor_tensor(total[t][:], sq_g[t][:], sq_win[t][:], ALU.add)
-        for c in range(2):
-            for t in range(PACK):
-                cols = slice(c * HALF, (c + 1) * HALF)
-                nc.vector.scalar_tensor_tensor(
-                    first[c][:, t, :], tab_g[t][:, cols], size[:, t : t + 1], a_win[t][:, cols], ALU.mult, ALU.add
-                )
-        for t in range(PACK):
-            gather_vector(a_g[0][:, t, :], a_win[t], half_of(n2_t, 0))
-        for c in range(2):
-            for t in range(PACK):
-                nc.scalar.activation(
-                    root[c][:, t, :], total[t][:, c * HALF : (c + 1) * HALF], ACT.Abs_reciprocal_sqrt, bias=0.25
-                )
-                gather_scalar(b_g[c][:, t, :], b_win[t], half_of(n4_t, c))
-        z_grouped0 = weave("z0", first[0], a_g[0], ALU.max)
-        for t in range(2):
-            gather_vector(a_g[1][:, t, :], a_win[t], half_of(n2_t, 1))
-        z_q = [quantised("z0", z_grouped0, HALF)]
-        z2_grouped0 = weave("y0", b_g[0], root[0], ALU.mult)
-        for t in range(2, PACK):
-            gather_scalar(a_g[1][:, t, :], a_win[t], half_of(n2_t, 1))
-        z2_q = [quantised("y0", z2_grouped0, HALF)]
-        z2_grouped1 = weave("y1", b_g[1], root[1], ALU.mult)
-        z_grouped1 = weave("z1", first[1], a_g[1], ALU.max)
-        z2_q.append(quantised("y1", z2_grouped1, HALF))
-        z_q.append(quantised("z1", z_grouped1, HALF))
+        REST = N - P
+        rest_codes = keep.tile([P, 2 * REST], U32, name="rest_codes", tag="first1", align_bytes=64)
+        rest_scale = sb("rest_scale", [P, 2 * REST], U8)
+        for number, grouped in enumerate((w2_grouped, w1_grouped)):
+            cols = slice(number * REST, (number + 1) * REST)
+            nc.vector.quantize_mx(out=rest_codes[:, cols].bitcast(FP8X4), scales=rest_scale[:, cols], in_=grouped[:, P * PACK :])
 
-        h_banks = []
+        def stationary(number, t):
+            if t == 0:
+                codes, scale = (w2_head, w1_head)[number]
+                return codes[:], scale[:]
+            cols = slice(number * REST + (t - 1) * P, number * REST + t * P)
+            return rest_codes[:, cols], rest_scale[:, cols]
+
+        def last_product(dst, t, c):
+            for number, moving in enumerate((z2_q, z_q)):
+                codes, scale = stationary(number, t)
+                nc.tensor.matmul_mx(
+                    dst, lhsT=codes.bitcast(FP8X4), lhsT_scale=scale,
+                    rhs=moving[c][0][:].bitcast(FP8X4), rhs_scale=moving[c][1][:],
+                    start=(number == 0), stop=(number == 1),
+                )
+
         h_win = [sb(f"h_win{t}", [P, S], F32) for t in range(PACK)]
         for c in range(2):
-            for t in range(PACK):
-                cols = slice(t * P, (t + 1) * P)
-                h_bank = psum.tile([P, HALF], F32, name=f"h_bank{c}{t}", tag=f"bank{(1 - c) * PACK + t}")
-                for number, (w_codes, w_scale, moving) in enumerate(((w2_codes, w2_scale, z2_q), (w1_codes, w1_scale, z_q))):
-                    nc.tensor.matmul_mx(
-                        h_bank[:], lhsT=w_codes[:, cols].bitcast(FP8X4), lhsT_scale=w_scale[:, cols],
-                        rhs=moving[c][0][:].bitcast(FP8X4), rhs_scale=moving[c][1][:],
-                        start=(number == 0), stop=(number == 1),
-                    )
-                if c == 0:
-                    nc.scalar.activation(h_win[t][:, :HALF], h_bank[:], ACT.Copy)
-                else:
-                    h_banks.append(h_bank)
+            h_half = psum.tile([P, HALF], F32, name=f"h_half{c}", tag=f"bank{c * PACK}")
+            last_product(h_half[:], 0, c)
+            nc.scalar.activation(h_win[0][:, cols_of(c)], h_half[:], ACT.Copy)
+        h_banks = [None]
+        for t in range(1, PACK):
+            h_banks.append(psum.tile([P, S], F32, name=f"h_bank{t}", tag=f"bank{t}"))
+            for c in range(2):
+                last_product(h_banks[t][:, cols_of(c)], t, c)
 
         out_rows = out.rearrange("(p t) j -> t p j", t=PACK)
-        pa, pb, inv, larger, result = [], [], [], [], []
-        for t in range(PACK):
-            nc.scalar.activation(h_win[t][:, HALF:], h_banks[t][:], ACT.Copy)
-            pa.append(sb(f"pa{t}", [P, W], F32))
-            pb.append(sb(f"pb{t}", [P, W], F32))
-            gather_scalar(pb[t][:], h_win[t], n6_t[:])
-            (gather_vector if t == 0 else gather_scalar)(pa[t][:], h_win[t], n5_t[:])
-            pb_size = sb(f"pb_size{t}", [P, W], F32)
-            nc.scalar.activation(pb_size[:], pb[t][:], ACT.Abs)
-            inv_root = sb(f"inv_root{t}", [P, W], F32)
-            nc.scalar.activation(inv_root[:], pb_size[:], ACT.Abs_reciprocal_sqrt, bias=0.5)
-            inv.append(sb(f"inv{t}", [P, W], F32))
-            nc.scalar.activation(inv[t][:], inv_root[:], ACT.Square)
-            larger.append(sb(f"larger{t}", [P, W], F32))
-            result.append(sb(f"result{t}", [P, S], F32))
+        pa = [sb(f"pa{t}", [P, W], F32) for t in range(PACK)]
+        pb = [sb(f"pb{t}", [P, W], F32) for t in range(PACK)]
+        pb_size = [sb(f"pb_size{t}", [P, W], F32) for t in range(PACK)]
+        inv_root = [sb(f"inv_root{t}", [P, W], F32) for t in range(PACK)]
+        inv = [sb(f"inv{t}", [P, W], F32) for t in range(PACK)]
+        larger = [sb(f"larger{t}", [P, W], F32) for t in range(PACK)]
+        result = [sb(f"result{t}", [P, S], F32) for t in range(PACK)]
 
-        def finish(t):
+        def fetch_steps(t):
+            return [
+                lambda: nc.scalar.activation(h_win[t][:], h_banks[t][:], ACT.Copy),
+                lambda: gather_scalar(pb[t][:], h_win[t], n6_t[:]),
+                lambda: gather_scalar(pa[t][:], h_win[t], n5_t[:]),
+            ]
+
+        def inverse_steps(t):
+            return [
+                lambda: nc.scalar.activation(pb_size[t][:], pb[t][:], ACT.Abs),
+                lambda: nc.scalar.activation(inv_root[t][:], pb_size[t][:], ACT.Abs_reciprocal_sqrt, bias=0.5),
+                lambda: nc.scalar.activation(inv[t][:], inv_root[t][:], ACT.Square),
+            ]
+
+        def put_larger(t):
+            nc.vector.tensor_copy(result[t][:].indirect(n6_t[:]), larger[t][:])
+
+        def put_ratio(t):
             nc.vector.tensor_tensor(result[t][:].indirect(n5_t[:]), pa[t][:], inv[t][:], ALU.mult)
             nc.sync.dma_start(out_rows[t], result[t][:])
 
-        for t in range(PACK):
+        def take_larger(t):
             nc.vector.tensor_tensor(larger[t][:], pa[t][:], pb[t][:], ALU.max)
-            if t > 0:
-                finish(t - 1)
-            nc.vector.tensor_copy(result[t][:].indirect(n6_t[:]), larger[t][:])
-        finish(PACK - 1)
+
+        gather_scalar(pb[0][:], h_win[0], n6_t[:])
+        gather_vector(pa[0][:], h_win[0], n5_t[:])
+        take_larger(0)
+        put_larger(0)
+        for invert, fetch in zip(inverse_steps(0), fetch_steps(1)):
+            invert()
+            fetch()
+        put_ratio(0)
+        take_larger(1)
+        put_larger(1)
+        for t in range(2, PACK):
+            for fetch, invert in zip(fetch_steps(t), inverse_steps(t - 1)):
+                fetch()
+                invert()
+            take_larger(t)
+            put_ratio(t - 1)
+            put_larger(t)
+        for invert in inverse_steps(PACK - 1):
+            invert()
+        put_ratio(PACK - 1)

@@ -46,42 +46,47 @@ def tile_picked_pqjkindrmsratio_none_p_kernel(
         nc.scalar.activation(warm[:, 1:2], warm[:, 0:1], ACT.Abs_reciprocal_sqrt, bias=0.25)
         d_byte_win = sb("d_byte_win", [P, G], U8)
         x_byte_win = sb("x_byte_win", [P, T], U8)
-        nc.vector.memset(d_byte_win[:].bitcast(I32), 0)
         nc.vector.memset(x_byte_win[:].bitcast(I32), 0)
+        nc.vector.memset(d_byte_win[:].bitcast(I32), 0)
         tab_rows = tab.rearrange("(p t) j -> t p j", t=PACK)
-        tab_win = [sb(f"tab_win{t}", [P, S], F32) for t in range(PACK)]
+        tab_win = [sb(f"tab_win{t}", [P, S], F32) for t in range(PACK - 1)]
         gm_t = sb("gm_t", [P, PACK], F32)
         nc.gpsimd.dma_start(gm_t[:], gm.rearrange("(p t) o -> p (t o)", t=PACK))
         gn_t = sb("gn_t", [P, PACK], F32)
         nc.gpsimd.dma_start(gn_t[:], gn.rearrange("(p t) o -> p (t o)", t=PACK))
-        k2_t = load_list("k2_t", k2)
         two_t = load_list("two_t", two)
+        k2_t = load_list("k2_t", k2)
         n1_t = load_list("n1_t", n1)
-        nc.sync.dma_start(d_byte_win[0:P:8, :].bitcast(I32), d_scales[0].bitcast(I32))
         nc.sync.dma_start(x_byte_win[0:P:8, :].bitcast(I32), x_scales[0].bitcast(I32))
+        nc.sync.dma_start(d_byte_win[0:P:8, :].bitcast(I32), d_scales[0].bitcast(I32))
         nc.sync.dma_start(tab_win[0][:], tab_rows[0])
         d_word_win = sb("d_word_win", [P, G], I32)
         nc.sync.dma_start(d_word_win[:], d_words[0].rearrange("p c r -> p (c r)").bitcast(I32))
         nc.sync.dma_start(tab_win[1][:], tab_rows[1])
+        n3_t = load_list("n3_t", n3)
+        n2_t = load_list("n2_t", n2)
+        n4_t = load_list("n4_t", n4)
+        n5_t = load_list("n5_t", n5)
         x_word_win = sb("x_word_win", [P, T], I32)
         nc.sync.dma_start(x_word_win[:], x_words[0].rearrange("p c r -> p (c r)").bitcast(I32))
+        nc.sync.dma_start(tab_win[2][:], tab_rows[2])
         k1_t = load_list("k1_t", k1)
         offs_t = load_list("offs_t", offs)
-        n3_t = load_list("n3_t", n3)
-        nc.sync.dma_start(tab_win[2][:], tab_rows[2])
 
-        def picked_scales(name, codes_t, tokens_t, queues):
-            d_bytes = sb(name + "_d_bytes", [P, H], U8)
-            nc.vector.tensor_copy(d_bytes[:], d_byte_win[:].indirect(codes_t[:]))
-            x_bytes = keep.tile([P, S], U8, name=name + "_x_bytes", tag=name + "_shared", align_bytes=64)
-            nc.vector.tensor_copy(x_bytes[:], x_byte_win[:].indirect(tokens_t[:]))
+        def picked_scales(name, codes_t, tokens_t):
             scale = sb(name + "_scale", [P, H + S], U8)
+            nc.gpsimd.memset(scale[:].bitcast(I32), 0)
+            x_bytes = sb(name + "_x_bytes", [P, S], U8)
+            nc.vector.tensor_copy(x_bytes[:], x_byte_win[:].indirect(tokens_t[:]))
+            d_bytes = keep.tile([P, H], U8, name=name + "_d_bytes", tag=name + "_d_bytes", align_bytes=64)
+            nc.vector.tensor_copy(d_bytes[:], d_byte_win[:].indirect(codes_t[:]))
+            joined = sb(name + "_joined", [P, H + S], U8)
+            nc.vector.tensor_copy(joined[:, H:].bitcast(I32), x_bytes[:].bitcast(I32))
             nc.vector.tensor_copy(
-                scale[:, :H].rearrange("p (t m) -> p t m", t=PACK), d_bytes[:].rearrange("p (m t) -> p t m", t=PACK)
+                joined[:, :H].rearrange("p (t m) -> p t m", t=PACK), d_bytes[:].rearrange("p (m t) -> p t m", t=PACK)
             )
-            nc.vector.tensor_copy(scale[:, H:].bitcast(I32), x_bytes[:].bitcast(I32))
-            for r in range(1, 4):
-                queues[r - 1].dma_start(scale[r:P:32, :].bitcast(I32), scale[8 * r : P : 32, :].bitcast(I32))
+            for r in range(4):
+                nc.sync.dma_start(scale[r:P:32, :].bitcast(I32), joined[8 * r : P : 32, :].bitcast(I32))
             return scale
 
         def load_weight(name, src, tag):
@@ -90,16 +95,13 @@ def tile_picked_pqjkindrmsratio_none_p_kernel(
             nc.sync.dma_start(raw, src.rearrange("(p j) m -> p j m", j=PACK))
             return raw
 
-        b_scale = picked_scales("b", k2_t, two_t, (nc.gpsimd, nc.scalar, nc.scalar))
+        b_scale = picked_scales("b", k2_t, two_t)
+        tab_win.append(keep.tile([P, S], F32, name="tab_win3", tag="b_d_bytes", align_bytes=64))
         nc.sync.dma_start(tab_win[3][:], tab_rows[3])
-        w1_raw = load_weight("w1_raw", w1, "b_shared")
-        n2_t = load_list("n2_t", n2)
-        n4_t = load_list("n4_t", n4)
-        n5_t = load_list("n5_t", n5)
         n6_t = load_list("n6_t", n6)
 
         def coded_product(name, number, scale, codes_t, tokens_t):
-            d_picked = sb(name + "_d_picked", [P, H], U32)
+            d_picked = keep.tile([P, H], U32, name=name + "_d_picked", tag=name + "_picked", align_bytes=64)
             nc.vector.tensor_copy(d_picked[:], d_word_win[:].bitcast(U32).indirect(codes_t[:]))
             x_picked = sb(name + "_x_picked", [P, S], U32)
             nc.vector.tensor_copy(x_picked[:], x_word_win[:].bitcast(U32).indirect(tokens_t[:]))
@@ -132,6 +134,7 @@ def tile_picked_pqjkindrmsratio_none_p_kernel(
         for t in range(PACK):
             gather_tab(t)
         b_banks = coded_product("b", 0, b_scale, k2_t, two_t)
+        w1_raw = load_weight("w1_raw", w1, "b_picked")
 
         identity = sb("identity", [P, P], F32)
         make_identity(nc, identity[:])
@@ -146,11 +149,10 @@ def tile_picked_pqjkindrmsratio_none_p_kernel(
         size16 = sb("size16", [P, PACK], F32)
         nc.gpsimd.tensor_scalar(size16[:], size[:], 0.0625, 0.0, ALU.mult, ALU.add)
 
-        a_scale = picked_scales("a", k1_t, offs_t, (nc.sync, nc.sync, nc.sync))
-        w2_raw = load_weight("w2_raw", w2, "a_shared")
+        a_scale = picked_scales("a", k1_t, offs_t)
         a_banks = coded_product("a", 1, a_scale, k1_t, offs_t)
+        w2_raw = load_weight("w2_raw", w2, "a_picked")
 
-        w2_grouped = sb("w2_grouped", [P, N * PACK], BF16)
         w1_grouped = sb("w1_grouped", [P, N * PACK], BF16)
         PIECE = 64
         for t in range(PACK):
@@ -161,16 +163,9 @@ def tile_picked_pqjkindrmsratio_none_p_kernel(
                     sign[:].unsqueeze(1).to_broadcast([P, PIECE, PACK]),
                     ALU.mult,
                 )
-        for t in range(PACK):
-            for m0 in range(0, P, PIECE):
-                nc.gpsimd.tensor_scalar(
-                    w2_grouped[:].rearrange("p (t m j) -> p t m j", t=PACK, j=PACK)[:, t, m0 : m0 + PIECE],
-                    w2_raw.rearrange("p j (m t) -> p t m j", t=PACK)[:, t, m0 : m0 + PIECE],
-                    1.0, 0.0, ALU.mult, ALU.add,
-                )
 
-        def quantised(name, grouped, width):
-            codes = sb(name + "_codes", [P, width], U32)
+        def quantised(name, grouped, width, tag=None):
+            codes = keep.tile([P, width], U32, name=name + "_codes", tag=tag or name + "_codes", align_bytes=64)
             scale = sb(name + "_scale", [P, width], U8)
             nc.vector.quantize_mx(out=codes[:].bitcast(FP8X4), scales=scale[:], in_=grouped)
             return codes, scale
@@ -186,14 +181,14 @@ def tile_picked_pqjkindrmsratio_none_p_kernel(
         def cols_of(c):
             return slice(c * HALF, (c + 1) * HALF)
 
-        sq_win = [sb(f"sq_win{t}", [P, S], F32) for t in range(PACK)]
-        b_win = [sb(f"b_win{t}", [P, S], F32) for t in range(PACK)]
-        sq_g = [sb(f"sq_g{t}", [P, S], F32) for t in range(PACK)]
-        a_win = [sb(f"a_win{t}", [P, S], F32) for t in range(PACK)]
+        sq_win = [keep.tile([P, S], F32, name=f"sq_win{t}", tag=f"sq_win{t}", align_bytes=64) for t in range(PACK)]
+        b_win = [keep.tile([P, S], F32, name=f"b_win{t}", tag=f"b_win{t}", align_bytes=64) for t in range(PACK)]
+        sq_g = [keep.tile([P, S], F32, name=f"sq_g{t}", tag=f"sq_g{t}", align_bytes=64) for t in range(PACK)]
+        a_win = [keep.tile([P, S], F32, name=f"a_win{t}", tag=f"a_win{t}", align_bytes=64) for t in range(PACK)]
         a_g = [sb("a_g0", [P, PACK, HALF], F32)]
-        b_g = [sb(f"b_g{c}", [P, PACK, HALF], F32) for c in range(2)]
+        b_g = [sb("b_g0", [P, PACK, HALF], F32)]
 
-        z_grouped = [sb(f"z_grouped{c}", [P, HALF * PACK], BF16) for c in range(2)]
+        z_grouped = [sb("z_grouped0", [P, HALF * PACK], BF16)]
         z2_grouped = [sb(f"z2_grouped{c}", [P, HALF * PACK], BF16) for c in range(2)]
         root_turned = [sb(f"root_turned{t}", [P, S], F32) for t in range(PACK)]
 
@@ -201,7 +196,7 @@ def tile_picked_pqjkindrmsratio_none_p_kernel(
             return slice(u * P, (u + 1) * P)
 
         def make_root(t):
-            total = psum.tile([P, S], F32, name=f"total{t}", tag=f"bank{t}")
+            total = psum.tile([P, S], F32, name=f"total{t}", tag=f"bank{PACK + t}")
             for u in range(PACK):
                 for number, term in enumerate((sq_win[t], sq_g[t])):
                     nc.tensor.matmul(
@@ -228,27 +223,34 @@ def tile_picked_pqjkindrmsratio_none_p_kernel(
             (gather_vector if t < 3 else gather_scalar)(a_g[0][:, t, :], a_win[t], half_of(n2_t, 0))
         for t in range(PACK):
             make_root(t)
-        root = [psum.tile([P, PACK, P], F32, name=f"root{u}", tag=f"bank{PACK + u}") for u in range(PACK)]
+        w2_by_tile = w2_raw.rearrange("p j (m t) -> p m j t", t=PACK)
+        w2_first = keep.tile([P, P * PACK], BF16, name="w2_first", tag="sq_g2", align_bytes=64)
+        nc.vector.tensor_copy(w2_first[:].rearrange("p (m j) -> p m j", j=PACK), w2_by_tile[:, :, :, 0])
+        root = [psum.tile([P, PACK, P], F32, name=f"root{u}", tag=f"bank{u}") for u in range(PACK)]
         for u in range(PACK):
             for t in range(PACK):
                 nc.tensor.transpose(root[u][:, t, :], root_turned[t][:, block(u)], identity[:])
-        first = keep.tile([P, PACK, S], F32, name="first", tag="first1", align_bytes=64)
+        first = sb("first", [P, PACK, S], F32)
         for t in range(PACK):
             nc.vector.scalar_tensor_tensor(first[:, t, :], tab_g[t][:], size[:, t : t + 1], a_win[t][:], ALU.mult, ALU.add)
         weave(z_grouped[0][:], first[:, :, :HALF], a_g[0][:], ALU.max)
         z_q = [quantised("z0", z_grouped[0][:], HALF)]
-        w1_head = quantised("w1_head", w1_grouped[:, : P * PACK], P)
+        w1_head = quantised("w1_head", w1_grouped[:, : P * PACK], P, "sq_win3")
         weave_z2(0)
-        w2_head = quantised("w2_head", w2_grouped[:, : P * PACK], P)
+        w2_head = quantised("w2_head", w2_first[:], P)
         z2_q = [quantised("y0", z2_grouped[0][:], HALF)]
+        b_g.append(keep.tile([P, PACK, HALF], F32, name="b_g1", tag="sq_g3", align_bytes=64))
         for t in range(PACK):
             gather_scalar(b_g[1][:, t, :], b_win[t], half_of(n4_t, 1))
-        a_late = [sb(f"a_late{v}", [P, PACK, P], F32) for v in range(2)]
+        a_late = [keep.tile([P, PACK, P], F32, name=f"a_late{v}", tag=tag, align_bytes=64) for v, tag in enumerate(("b_win3", "b_win2"))]
         for v in range(2):
             for t in range(PACK):
                 gather_scalar(a_late[v][:, t, :], a_win[t], n2_t[:, (HALF + v * P) // GROUP : (HALF + (v + 1) * P) // GROUP])
+        w2_rest = keep.tile([P, (N - P) * PACK], BF16, name="w2_rest", tag=f"a_win{PACK - 1}", align_bytes=64)
+        nc.scalar.activation(w2_rest[:].rearrange("p (t m j) -> p m j t", t=PACK - 1, j=PACK), w2_by_tile[:, :, :, 1:], ACT.Copy)
         weave_z2(1)
         z2_q.append(quantised("y1", z2_grouped[1][:], HALF))
+        z_grouped.append(keep.tile([P, HALF * PACK], BF16, name="z_grouped1", tag="sq_g3", align_bytes=64))
         z1_codes = sb("z1_codes", [P, HALF], U32)
         z1_scale = sb("z1_scale", [P, HALF], U8)
         for v in range(2):
@@ -260,11 +262,11 @@ def tile_picked_pqjkindrmsratio_none_p_kernel(
         z_q.append((z1_codes, z1_scale))
 
         REST = N - P
-        rest_codes = keep.tile([P, 2 * REST], U32, name="rest_codes", tag="first1", align_bytes=64)
+        rest_codes = keep.tile([P, 2 * REST], U32, name="rest_codes", tag="sq_g3", align_bytes=64)
         rest_scale = sb("rest_scale", [P, 2 * REST], U8)
-        for number, grouped in enumerate((w2_grouped, w1_grouped)):
+        for number, grouped in ((1, w1_grouped[:, P * PACK :]), (0, w2_rest[:])):
             cols = slice(number * REST, (number + 1) * REST)
-            nc.vector.quantize_mx(out=rest_codes[:, cols].bitcast(FP8X4), scales=rest_scale[:, cols], in_=grouped[:, P * PACK :])
+            nc.vector.quantize_mx(out=rest_codes[:, cols].bitcast(FP8X4), scales=rest_scale[:, cols], in_=grouped)
 
         def stationary(number, t):
             if t == 0:
@@ -284,12 +286,12 @@ def tile_picked_pqjkindrmsratio_none_p_kernel(
 
         h_win = [sb(f"h_win{t}", [P, S], F32) for t in range(PACK)]
         for c in range(2):
-            h_half = psum.tile([P, HALF], F32, name=f"h_half{c}", tag=f"bank{c * PACK}")
+            h_half = psum.tile([P, HALF], F32, name=f"h_half{c}", tag=f"bank{PACK + c}")
             last_product(h_half[:], 0, c)
             nc.scalar.activation(h_win[0][:, cols_of(c)], h_half[:], ACT.Copy)
         h_banks = [None]
         for t in range(1, PACK):
-            h_banks.append(psum.tile([P, S], F32, name=f"h_bank{t}", tag=f"bank{t}"))
+            h_banks.append(psum.tile([P, S], F32, name=f"h_bank{t}", tag=f"bank{(PACK + 1 + t) % (2 * PACK)}"))
             for c in range(2):
                 last_product(h_banks[t][:, cols_of(c)], t, c)
 

from contextlib import ExitStack

import concourse.mybir as mybir
from concourse.masks import make_identity

F32 = mybir.dt.float32
BF16 = mybir.dt.bfloat16
I32 = mybir.dt.int32
U32 = mybir.dt.uint32
U16 = mybir.dt.uint16
U8 = mybir.dt.uint8
FP8X4 = mybir.dt.float8_e4m3fn_x4
ALU = mybir.AluOpType
ACT = mybir.ActivationFunctionType

P = 128
PACK = 4
K, T, G, H, S, N, W = 512, 1024, 2048, 512, 512, 512, 256
HALF = S // 2
GROUP = 16
FLOPS = 4 * 2 * 512 * 512 * 512


def tile_picked_pqjkindrmsratio_none_p_kernel(
    tc, x_words, x_scales, d_words, d_scales, tab, gn, gm, w1, w2, offs, k1, two, k2, n1, n2, n3, n4, n5, n6, out
):
    nc = tc.nc
    with ExitStack() as ctx:
        lists = ctx.enter_context(tc.tile_pool(name="lists", bufs=1))
        keep = ctx.enter_context(tc.tile_pool(name="keep", bufs=1))
        psum = ctx.enter_context(tc.psum_pool(name="psum", bufs=1))

        def sb(name, shape, dtype):
            return keep.tile(shape, dtype, name=name, align_bytes=64)

        def load_list(name, src):
            tile = lists.tile([P, src.shape[1]], U16, name=name)
            nc.sync.dma_start(tile[:], src)
            return tile

        def half_of(tile, c):
            return tile[:, c * (HALF // GROUP) : (c + 1) * (HALF // GROUP)]

        warm = sb("warm", [P, 2], F32)
        nc.gpsimd.memset(warm[:, 0:1], 1.0)
        nc.scalar.activation(warm[:, 1:2], warm[:, 0:1], ACT.Abs_reciprocal_sqrt, bias=0.25)
        d_byte_win = sb("d_byte_win", [P, G], U8)
        x_byte_win = sb("x_byte_win", [P, T], U8)
        nc.vector.memset(x_byte_win[:].bitcast(I32), 0)
        nc.vector.memset(d_byte_win[:].bitcast(I32), 0)
        tab_rows = tab.rearrange("(p t) j -> t p j", t=PACK)
        tab_win = [sb(f"tab_win{t}", [P, S], F32) for t in range(PACK - 1)]
        gm_t = sb("gm_t", [P, PACK], F32)
        nc.gpsimd.dma_start(gm_t[:], gm.rearrange("(p t) o -> p (t o)", t=PACK))
        gn_t = sb("gn_t", [P, PACK], F32)
        nc.gpsimd.dma_start(gn_t[:], gn.rearrange("(p t) o -> p (t o)", t=PACK))
        two_t = load_list("two_t", two)
        k2_t = load_list("k2_t", k2)
        n1_t = load_list("n1_t", n1)
        nc.sync.dma_start(x_byte_win[0:P:8, :].bitcast(I32), x_scales[0].bitcast(I32))
        nc.sync.dma_start(d_byte_win[0:P:8, :].bitcast(I32), d_scales[0].bitcast(I32))
        nc.sync.dma_start(tab_win[0][:], tab_rows[0])
        d_word_win = sb("d_word_win", [P, G], I32)
        nc.sync.dma_start(d_word_win[:], d_words[0].rearrange("p c r -> p (c r)").bitcast(I32))
        nc.sync.dma_start(tab_win[1][:], tab_rows[1])
        n3_t = load_list("n3_t", n3)
        n2_t = load_list("n2_t", n2)
        n4_t = load_list("n4_t", n4)
        n5_t = load_list("n5_t", n5)
        x_word_win = sb("x_word_win", [P, T], I32)
        nc.sync.dma_start(x_word_win[:], x_words[0].rearrange("p c r -> p (c r)").bitcast(I32))
        nc.sync.dma_start(tab_win[2][:], tab_rows[2])
        k1_t = load_list("k1_t", k1)
        offs_t = load_list("offs_t", offs)

        def picked_scales(name, codes_t, tokens_t):
            scale = sb(name + "_scale", [P, H + S], U8)
            nc.gpsimd.memset(scale[:].bitcast(I32), 0)
            x_bytes = sb(name + "_x_bytes", [P, S], U8)
            nc.vector.tensor_copy(x_bytes[:], x_byte_win[:].indirect(tokens_t[:]))
            d_bytes = keep.tile([P, H], U8, name=name + "_d_bytes", tag=name + "_d_bytes", align_bytes=64)
            nc.vector.tensor_copy(d_bytes[:], d_byte_win[:].indirect(codes_t[:]))
            joined = sb(name + "_joined", [P, H + S], U8)
            nc.vector.tensor_copy(joined[:, H:].bitcast(I32), x_bytes[:].bitcast(I32))
            nc.vector.tensor_copy(
                joined[:, :H].rearrange("p (t m) -> p t m", t=PACK), d_bytes[:].rearrange("p (m t) -> p t m", t=PACK)
            )
            for r in range(4):
                nc.sync.dma_start(scale[r:P:32, :].bitcast(I32), joined[8 * r : P : 32, :].bitcast(I32))
            return scale

        def load_weight(name, src, tag):
            tile = keep.tile([P, PACK * N], F32, name=name, tag=tag, align_bytes=64)
            raw = tile[:].rearrange("p (j m) -> p j m", j=PACK)
            nc.sync.dma_start(raw, src.rearrange("(p j) m -> p j m", j=PACK))
            return raw

        b_scale = picked_scales("b", k2_t, two_t)
        tab_win.append(keep.tile([P, S], F32, name="tab_win3", tag="b_d_bytes", align_bytes=64))
        nc.sync.dma_start(tab_win[3][:], tab_rows[3])
        n6_t = load_list("n6_t", n6)

        def coded_product(name, number, scale, codes_t, tokens_t):
            d_picked = keep.tile([P, H], U32, name=name + "_d_picked", tag=name + "_picked", align_bytes=64)
            nc.vector.tensor_copy(d_picked[:], d_word_win[:].bitcast(U32).indirect(codes_t[:]))
            x_picked = sb(name + "_x_picked", [P, S], U32)
            nc.vector.tensor_copy(x_picked[:], x_word_win[:].bitcast(U32).indirect(tokens_t[:]))
            d_dealt = sb(name + "_d_dealt", [P, H], U32)
            nc.vector.tensor_copy(
                d_dealt[:].rearrange("p (t m) -> p m t", t=PACK), d_picked[:].rearrange("p (m t) -> p m t", t=PACK)
            )
            banks = []
            for t in range(PACK):
                bank = psum.tile([P, S], F32, name=f"{name}_bank{t}", tag=f"bank{number * PACK + t}")
                nc.tensor.matmul_mx(
                    bank[:], lhsT=d_dealt[:, t * P : (t + 1) * P].bitcast(FP8X4), lhsT_scale=scale[:, t * P : (t + 1) * P],
                    rhs=x_picked[:].bitcast(FP8X4), rhs_scale=scale[:, H:], start=True, stop=True,
                )
                banks.append(bank)
            return banks

        def gather_scalar(dst, window, offsets):
            nc.scalar.activation(dst, window[:].indirect(offsets), ACT.Copy)

        def gather_vector(dst, window, offsets):
            nc.vector.tensor_copy(dst, window[:].indirect(offsets))

        tab_g = [sb(f"tab_g{t}", [P, S], F32) for t in range(PACK)]

        def gather_tab(t):
            for c in range(2):
                gather_scalar(tab_g[t][:, c * HALF : (c + 1) * HALF], tab_win[t], half_of(n1_t, c))

        for t in range(PACK):
            gather_tab(t)
        b_banks = coded_product("b", 0, b_scale, k2_t, two_t)
        w1_raw = load_weight("w1_raw", w1, "b_picked")

        identity = sb("identity", [P, P], F32)
        make_identity(nc, identity[:])
        gm16 = sb("gm16", [P, PACK], F32)
        nc.gpsimd.tensor_scalar(gm16[:], gm_t[:], 0.0625, 0.0, ALU.mult, ALU.add)
        sign = sb("sign", [P, PACK], F32)
        step = sb("step", [P, PACK], F32)
        nc.gpsimd.tensor_scalar(step[:], gn_t[:], 0.0, 2.0, ALU.is_ge, ALU.mult)
        nc.gpsimd.tensor_scalar(sign[:], step[:], 1.0, -1.0, ALU.mult, ALU.add)
        size = sb("size", [P, PACK], F32)
        nc.gpsimd.tensor_tensor(size[:], gn_t[:], sign[:], ALU.mult)
        size16 = sb("size16", [P, PACK], F32)
        nc.gpsimd.tensor_scalar(size16[:], size[:], 0.0625, 0.0, ALU.mult, ALU.add)

        a_scale = picked_scales("a", k1_t, offs_t)
        a_banks = coded_product("a", 1, a_scale, k1_t, offs_t)
        w2_raw = load_weight("w2_raw", w2, "a_picked")

        w1_grouped = sb("w1_grouped", [P, N * PACK], BF16)
        PIECE = 64
        for t in range(PACK):
            for m0 in range(0, P, PIECE):
                nc.gpsimd.tensor_tensor(
                    w1_grouped[:].rearrange("p (t m j) -> p t m j", t=PACK, j=PACK)[:, t, m0 : m0 + PIECE],
                    w1_raw.rearrange("p j (m t) -> p t m j", t=PACK)[:, t, m0 : m0 + PIECE],
                    sign[:].unsqueeze(1).to_broadcast([P, PIECE, PACK]),
                    ALU.mult,
                )

        def quantised(name, grouped, width, tag=None):
            codes = keep.tile([P, width], U32, name=name + "_codes", tag=tag or name + "_codes", align_bytes=64)
            scale = sb(name + "_scale", [P, width], U8)
            nc.vector.quantize_mx(out=codes[:].bitcast(FP8X4), scales=scale[:], in_=grouped)
            return codes, scale

        def weave(grouped, left, right, op):
            nc.vector.tensor_tensor(
                grouped.rearrange("p (c i t) -> p c t i", i=4, t=PACK),
                left.rearrange("p t (c i) -> p c t i", i=4),
                right.rearrange("p t (c i) -> p c t i", i=4),
                op,
            )

        def cols_of(c):
            return slice(c * HALF, (c + 1) * HALF)

        sq_win = [keep.tile([P, S], F32, name=f"sq_win{t}", tag=f"sq_win{t}", align_bytes=64) for t in range(PACK)]
        b_win = [keep.tile([P, S], F32, name=f"b_win{t}", tag=f"b_win{t}", align_bytes=64) for t in range(PACK)]
        sq_g = [keep.tile([P, S], F32, name=f"sq_g{t}", tag=f"sq_g{t}", align_bytes=64) for t in range(PACK)]
        a_win = [keep.tile([P, S], F32, name=f"a_win{t}", tag=f"a_win{t}", align_bytes=64) for t in range(PACK)]
        a_g = [sb("a_g0", [P, PACK, HALF], F32)]
        b_g = [sb("b_g0", [P, PACK, HALF], F32)]

        z_grouped = [sb("z_grouped0", [P, HALF * PACK], BF16)]
        z2_grouped = [sb(f"z2_grouped{c}", [P, HALF * PACK], BF16) for c in range(2)]
        root_turned = [sb(f"root_turned{t}", [P, S], F32) for t in range(PACK)]

        def block(u):
            return slice(u * P, (u + 1) * P)

        def make_root(t):
            total = psum.tile([P, S], F32, name=f"total{t}", tag=f"bank{PACK + t}")
            for u in range(PACK):
                for number, term in enumerate((sq_win[t], sq_g[t])):
                    nc.tensor.matmul(
                        total[:, block(u)], term[:, block(u)], identity[:], start=(number == 0), stop=(number == 1), is_transpose=True
                    )
            nc.scalar.activation(root_turned[t][:], total[:], ACT.Abs_reciprocal_sqrt, bias=0.25)

        def weave_z2(c):
            for v in range(2):
                weave(z2_grouped[c][:, v * P * PACK : (v + 1) * P * PACK], b_g[c][:, :, block(v)], root[2 * c + v][:], ALU.mult)

        for t in range(PACK):
            nc.scalar.activation(sq_win[t][:], b_banks[t][:], ACT.Square, scale=0.0625)
        for t in range(PACK):
            nc.scalar.activation(b_win[t][:], b_banks[t][:], ACT.Copy, scale=gm16[:, t : t + 1])
        for t in range(PACK):
            nc.scalar.activation(a_win[t][:], a_banks[t][:], ACT.Copy, scale=size16[:, t : t + 1])
        for t in range(PACK):
            for c in range(2):
                gather_vector(sq_g[t][:, cols_of(c)], sq_win[t], half_of(n3_t, c))
        for t in range(PACK):
            gather_scalar(b_g[0][:, t, :], b_win[t], half_of(n4_t, 0))
        for t in range(PACK):
            (gather_vector if t < 3 else gather_scalar)(a_g[0][:, t, :], a_win[t], half_of(n2_t, 0))
        for t in range(PACK):
            make_root(t)
        w2_by_tile = w2_raw.rearrange("p j (m t) -> p m j t", t=PACK)
        w2_first = keep.tile([P, P * PACK], BF16, name="w2_first", tag="sq_g2", align_bytes=64)
        nc.vector.tensor_copy(w2_first[:].rearrange("p (m j) -> p m j", j=PACK), w2_by_tile[:, :, :, 0])
        root = [psum.tile([P, PACK, P], F32, name=f"root{u}", tag=f"bank{u}") for u in range(PACK)]
        for u in range(PACK):
            for t in range(PACK):
                nc.tensor.transpose(root[u][:, t, :], root_turned[t][:, block(u)], identity[:])
        first = sb("first", [P, PACK, S], F32)
        for t in range(PACK):
            nc.vector.scalar_tensor_tensor(first[:, t, :], tab_g[t][:], size[:, t : t + 1], a_win[t][:], ALU.mult, ALU.add)
        weave(z_grouped[0][:], first[:, :, :HALF], a_g[0][:], ALU.max)
        z_q = [quantised("z0", z_grouped[0][:], HALF)]
        w1_head = quantised("w1_head", w1_grouped[:, : P * PACK], P, "sq_win3")
        weave_z2(0)
        w2_head = quantised("w2_head", w2_first[:], P)
        z2_q = [quantised("y0", z2_grouped[0][:], HALF)]
        b_g.append(keep.tile([P, PACK, HALF], F32, name="b_g1", tag="sq_g3", align_bytes=64))
        for t in range(PACK):
            gather_scalar(b_g[1][:, t, :], b_win[t], half_of(n4_t, 1))
        a_late = [keep.tile([P, PACK, P], F32, name=f"a_late{v}", tag=tag, align_bytes=64) for v, tag in enumerate(("b_win3", "b_win2"))]
        for v in range(2):
            for t in range(PACK):
                gather_scalar(a_late[v][:, t, :], a_win[t], n2_t[:, (HALF + v * P) // GROUP : (HALF + (v + 1) * P) // GROUP])
        w2_rest = keep.tile([P, (N - P) * PACK], BF16, name="w2_rest", tag=f"a_win{PACK - 1}", align_bytes=64)
        nc.scalar.activation(w2_rest[:].rearrange("p (t m j) -> p m j t", t=PACK - 1, j=PACK), w2_by_tile[:, :, :, 1:], ACT.Copy)
        weave_z2(1)
        z2_q.append(quantised("y1", z2_grouped[1][:], HALF))
        z_grouped.append(keep.tile([P, HALF * PACK], BF16, name="z_grouped1", tag="sq_g3", align_bytes=64))
        z1_codes = sb("z1_codes", [P, HALF], U32)
        z1_scale = sb("z1_scale", [P, HALF], U8)
        for v in range(2):
            weave(z_grouped[1][:, v * P * PACK : (v + 1) * P * PACK], first[:, :, block(2 + v)], a_late[v][:], ALU.max)
        for v in range(2):
            nc.vector.quantize_mx(
                out=z1_codes[:, block(v)].bitcast(FP8X4), scales=z1_scale[:, block(v)], in_=z_grouped[1][:, v * P * PACK : (v + 1) * P * PACK]
            )
        z_q.append((z1_codes, z1_scale))

        REST = N - P
        rest_codes = keep.tile([P, 2 * REST], U32, name="rest_codes", tag="sq_g3", align_bytes=64)
        rest_scale = sb("rest_scale", [P, 2 * REST], U8)
        for number, grouped in ((1, w1_grouped[:, P * PACK :]), (0, w2_rest[:])):
            cols = slice(number * REST, (number + 1) * REST)
            nc.vector.quantize_mx(out=rest_codes[:, cols].bitcast(FP8X4), scales=rest_scale[:, cols], in_=grouped)

        def stationary(number, t):
            if t == 0:
                codes, scale = (w2_head, w1_head)[number]
                return codes[:], scale[:]
            cols = slice(number * REST + (t - 1) * P, number * REST + t * P)
            return rest_codes[:, cols], rest_scale[:, cols]

        def last_product(dst, t, c):
            for number, moving in enumerate((z2_q, z_q)):
                codes, scale = stationary(number, t)
                nc.tensor.matmul_mx(
                    dst, lhsT=codes.bitcast(FP8X4), lhsT_scale=scale,
                    rhs=moving[c][0][:].bitcast(FP8X4), rhs_scale=moving[c][1][:],
                    start=(number == 0), stop=(number == 1),
                )

        h_win = [sb(f"h_win{t}", [P, S], F32) for t in range(PACK)]
        for c in range(2):
            h_half = psum.tile([P, HALF], F32, name=f"h_half{c}", tag=f"bank{PACK + c}")
            last_product(h_half[:], 0, c)
            nc.scalar.activation(h_win[0][:, cols_of(c)], h_half[:], ACT.Copy)
        h_banks = [None]
        for t in range(1, PACK):
            h_banks.append(psum.tile([P, S], F32, name=f"h_bank{t}", tag=f"bank{(PACK + 1 + t) % (2 * PACK)}"))
            for c in range(2):
                last_product(h_banks[t][:, cols_of(c)], t, c)

        out_rows = out.rearrange("(p t) j -> t p j", t=PACK)
        pa = [sb(f"pa{t}", [P, W], F32) for t in range(PACK)]
        pb = [sb(f"pb{t}", [P, W], F32) for t in range(PACK)]
        pb_size = [sb(f"pb_size{t}", [P, W], F32) for t in range(PACK)]
        inv_root = [sb(f"inv_root{t}", [P, W], F32) for t in range(PACK)]
        inv = [sb(f"inv{t}", [P, W], F32) for t in range(PACK)]
        larger = [sb(f"larger{t}", [P, W], F32) for t in range(PACK)]
        result = [sb(f"result{t}", [P, S], F32) for t in range(PACK)]

        def fetch_steps(t):
            return [
                lambda: nc.scalar.activation(h_win[t][:], h_banks[t][:], ACT.Copy),
                lambda: gather_scalar(pb[t][:], h_win[t], n6_t[:]),
                lambda: gather_scalar(pa[t][:], h_win[t], n5_t[:]),
            ]

        def inverse_steps(t):
            return [
                lambda: nc.scalar.activation(pb_size[t][:], pb[t][:], ACT.Abs),
                lambda: nc.scalar.activation(inv_root[t][:], pb_size[t][:], ACT.Abs_reciprocal_sqrt, bias=0.5),
                lambda: nc.scalar.activation(inv[t][:], inv_root[t][:], ACT.Square),
            ]

        def put_larger(t):
            nc.vector.tensor_copy(result[t][:].indirect(n6_t[:]), larger[t][:])

        def put_ratio(t):
            nc.vector.tensor_tensor(result[t][:].indirect(n5_t[:]), pa[t][:], inv[t][:], ALU.mult)
            nc.sync.dma_start(out_rows[t], result[t][:])

        def take_larger(t):
            nc.vector.tensor_tensor(larger[t][:], pa[t][:], pb[t][:], ALU.max)

        gather_scalar(pb[0][:], h_win[0], n6_t[:])
        gather_vector(pa[0][:], h_win[0], n5_t[:])
        take_larger(0)
        put_larger(0)
        for invert, fetch in zip(inverse_steps(0), fetch_steps(1)):
            invert()
            fetch()
        put_ratio(0)
        take_larger(1)
        put_larger(1)
        for t in range(2, PACK):
            for fetch, invert in zip(fetch_steps(t), inverse_steps(t - 1)):
                fetch()
                invert()
            take_larger(t)
            put_ratio(t - 1)
            put_larger(t)
        for invert in inverse_steps(PACK - 1):
            invert()
        put_ratio(PACK - 1)
